import numpy as np
import ml_dtypes


def mxq(x, axis, fmt="e4m3"):
    dtype, down = {"e4m3": (ml_dtypes.float8_e4m3fn, 7), "e5m2": (ml_dtypes.float8_e5m2, 14)}[fmt]
    v = np.moveaxis(np.asarray(x, np.float32).astype(ml_dtypes.bfloat16).astype(np.float64), axis, -1)
    blocks = v.reshape(v.shape[:-1] + (-1, 32))
    amax = np.abs(blocks).max(-1, keepdims=True)
    byte = np.maximum(np.where(amax > 0, np.frexp(amax)[1] - 1 + 127, 0) - down, 1)
    scale = np.exp2(byte - 127.0)
    codes = (blocks / scale).astype(np.float32).astype(dtype).astype(np.float64)
    return np.moveaxis((codes * scale).reshape(v.shape), -1, axis)


WIDE = False


def mx_kscale(k):
    if not WIDE:
        return np.ones(k)
    levels = np.array([10, -10, 5, -5, 0])
    if k % 512:
        return np.exp2(np.random.permutation(np.resize(levels, k // 32))).repeat(32)
    a = np.empty((k // 512, 16))
    for p in range(k // 512):
        a[p, :8] = np.random.permutation(np.resize(levels, 8))
        for g in range(8):
            far = levels[np.abs(levels - a[p, g]) >= 10]
            a[p, g + 8] = far[np.random.randint(len(far))]
    return np.exp2(a.ravel()).repeat(32)


def f64(x):
    return np.asarray(x).astype(np.float64)


def striped(idx):
    return np.tile(idx.reshape(-1, 16).T, (8, 1)).astype(np.uint16)


def unstriped(offs):
    return offs[:16].T.reshape(-1).astype(np.int64)


def striped8(idx):
    return np.concatenate([x.reshape(-1, 16).T for x in idx]).astype(np.uint16)


def runs(offs, k):
    lists = np.stack([offs[16 * r : 16 * r + 16].T.reshape(-1) for r in range(8)]).astype(np.int64)
    return lists[np.arange(k) % 512 // 64]


def pack_weight(w):
    k, n = w.shape
    w = f64(np.asarray(w, np.float32).astype(ml_dtypes.bfloat16)).reshape(k // 32, 32, n)
    amax = np.abs(w).max(1)
    byte = np.clip(np.where(amax > 0, np.frexp(amax)[1] - 1 + 127 - 7, 1), 1, 254)
    scaled = (w * np.exp2(127.0 - byte)[:, None, :]).reshape(k, n).astype(np.float32)
    words = np.ascontiguousarray(scaled.reshape(k // 512, 128, 4, n).transpose(0, 1, 3, 2)).astype(ml_dtypes.float8_e4m3fn).view(np.uint8)
    return words, np.ascontiguousarray(byte.astype(np.uint8).reshape(k // 512, 16, n))


def unpack_weight(words, scales):
    g, p, n, _ = words.shape
    vals = np.ascontiguousarray(words).view(ml_dtypes.float8_e4m3fn).astype(np.float64) * np.repeat(np.exp2(scales.astype(np.float64) - 127.0), 8, axis=1)[..., None]
    return vals.transpose(0, 1, 3, 2).reshape(g * 512, n)


def sigmoid(v):
    return 1.0 / (1.0 + np.exp(-np.maximum(v, -700.0)))

def planes(y):
    n, m = y.shape
    v = y.astype(np.float32).astype(ml_dtypes.bfloat16).astype(np.float64).reshape(n // 32, 32, m)
    top = np.abs(v).max(1)
    byte = np.clip(np.where(top > 0, np.frexp(top)[1] - 1 + 127 - 7, 1), 1, 254)
    codes = (v * np.exp2(127.0 - byte)[:, None, :]).reshape(n, m).astype(np.float32).astype(ml_dtypes.float8_e4m3fn).view(np.uint8)
    words = codes.reshape(n // 512, 128, 4, m).transpose(0, 1, 3, 2)
    return np.ascontiguousarray(words), np.ascontiguousarray(byte.astype(np.uint8).reshape(n // 512, 16, m))


K, T, S, G, H, W, U = 512, 2048, 256, 2048, 512, 128, 1024


def setup_inputs():
    n = np.random.standard_normal
    s = mx_kscale(K)[:, None]
    packed_xT = pack_weight(n((K, T)) * s)
    packed_dT = pack_weight(n((K, G)) / s)
    perm = np.random.permutation(S)
    return {
        "x_words": packed_xT[0],
        "x_scales": packed_xT[1],
        "d_words": packed_dT[0],
        "d_scales": packed_dT[1],
        "sl": np.random.uniform(1.0, 2.0, (H, 1)).astype(np.float32),
        "th": (0.5 * n((H, 1))).astype(np.float32),
        "gs": (np.random.uniform(0.5, 1.5, (K, 1)) * s).astype(np.float32),
        "mem": n((H, U)).astype(np.float32),
        "sl2": np.random.uniform(1.0, 2.0, (H, 1)).astype(np.float32),
        "th2": (0.5 * n((H, 1))).astype(np.float32),
        "offs": striped(np.random.permutation(T)[:S]),
        "k1": striped8(np.random.randint(0, G, (8, H))),
        "n1": striped(perm[:W]),
        "n2": striped(perm[W:]),
        "n3": striped(np.random.permutation(U)[:S]),
        "n4": striped(np.random.permutation(S)),
    }


def reference(x_words, x_scales, d_words, d_scales, sl, th, gs, mem, sl2, th2, offs, k1, n1, n2, n3, n4):
    old = f64(mem)[:, unstriped(n3)]
    d_k1 = unpack_weight(d_words, d_scales)[np.arange(K)[:, None], runs(k1, K)]
    xq = unpack_weight(x_words, x_scales)[:, unstriped(offs)]
    h = 0.0625 * (d_k1.T @ xq)
    pb = h[:, unstriped(n2)]
    sg = sigmoid(f64(sl) * (h[:, unstriped(n1)] - f64(th)))
    rb = pb - sg
    pa = h[:, unstriped(n1)]
    sg2 = sigmoid(f64(sl) * (h[:, unstriped(n2)] - f64(th)))
    ra = pa * sg2
    ds = np.zeros((H, S))
    ds[:, unstriped(n1)] = ra
    dt = ds.copy()
    dt[:, unstriped(n2)] = rb
    z = f64(gs) * dt
    h2 = 0.0625 * ((d_k1.T @ mxq(z, 0, "e4m3")))
    sg3 = sigmoid(f64(sl2) * (h2[:, unstriped(n4)] - f64(th2)))
    nw = old + sg3 * (h2 - old)
    out = f64(mem).copy()
    out[:, unstriped(n3)] = nw
    return (out,) + planes(out)

@@ -1,0 +1,219 @@
+from contextlib import ExitStack
+
+import concourse.mybir as mybir
+
+F32 = mybir.dt.float32
+BF16 = mybir.dt.bfloat16
+I32 = mybir.dt.int32
+U32 = mybir.dt.uint32
+U16 = mybir.dt.uint16
+U8 = mybir.dt.uint8
+FP8X4 = mybir.dt.float8_e4m3fn_x4
+MULT = mybir.AluOpType.mult
+ADD = mybir.AluOpType.add
+SUB = mybir.AluOpType.subtract
+COPY = mybir.ActivationFunctionType.Copy
+SIGMOID = mybir.ActivationFunctionType.Sigmoid
+
+P = 128
+PACK = 4
+T = 2048
+S = 256
+H = 512
+W = 128
+U = 1024
+HALF = U // 2
+FLOPS = 2 * 2 * 512 * H * S
+
+
+def words_of(dram):
+    return dram[0].rearrange("p c r -> p (c r)").bitcast(I32)
+
+
+def tile_picked_ringeodepg_none_po_kernel(
+    tc, x_words, x_scales, d_words, d_scales, sl, th, gs, mem, sl2, th2, offs, k1, n1, n2, n3, n4, out_0, out_1, out_2
+):
+    nc = tc.nc
+    with ExitStack() as ctx:
+        lists = ctx.enter_context(tc.tile_pool(name="lists", bufs=1))
+        pool = ctx.enter_context(tc.tile_pool(name="pool", bufs=1))
+        psum = ctx.enter_context(tc.psum_pool(name="psum", bufs=1))
+
+        def load_list(dram, name):
+            tile = lists.tile(list(dram.shape), U16, name=name)
+            nc.sync.dma_start(tile[:], dram)
+            return tile
+
+        def load_rows(dram, name):
+            tile = pool.tile([P, PACK], F32, name=name)
+            nc.gpsimd.dma_start(tile[:], dram.rearrange("(p t) o -> p (t o)", t=PACK))
+            return tile
+
+        d_scale_table = pool.tile([P, T], U8, name="d_scale_table", align_bytes=64)
+        d_scale_rows = d_scales[0].bitcast(I32).rearrange("(r e) c -> e r c", e=2)
+        for e in range(2):
+            nc.sync.dma_start(
+                d_scale_table[e:P:2, :].bitcast(I32), d_scale_rows[e].unsqueeze(1).to_broadcast([8, 8, T // 4])
+            )
+        k1_t = load_list(k1, "k1_t")
+        offs_t = load_list(offs, "offs_t")
+        n1_t = load_list(n1, "n1_t")
+        n2_t = load_list(n2, "n2_t")
+        n3_t = load_list(n3, "n3_t")
+        d_table = pool.tile([P, T], U32, name="d_table", tag="page3", align_bytes=64)
+        nc.sync.dma_start(d_table[:].bitcast(I32), words_of(d_words))
+        x_table = pool.tile([P, T], U32, name="x_table", tag="page1", align_bytes=64)
+        nc.sync.dma_start(x_table[:].bitcast(I32), words_of(x_words))
+        n4_t = load_list(n4, "n4_t")
+
+        x_scale_table = pool.tile([P, T], U8, name="x_scale_table", align_bytes=64)
+        nc.vector.memset(x_scale_table[:].bitcast(I32), 0)
+        x_scale_rows = x_scales[0].bitcast(I32)
+        for q in range(4):
+            nc.scalar.dma_start(x_scale_table[32 * q : 32 * q + 4, :].bitcast(I32), x_scale_rows[4 * q : 4 * q + 4, :])
+
+        d_scale = pool.tile([P, H], U8, name="d_scale", align_bytes=64)
+        nc.vector.memset(d_scale[:].bitcast(I32), 0)
+        z_scale = pool.tile([P, S], U8, name="z_scale", align_bytes=64)
+        nc.vector.memset(z_scale[:].bitcast(I32), 0)
+
+        sl_t = load_rows(sl, "sl_t")
+        th_t = load_rows(th, "th_t")
+        gs_t = load_rows(gs, "gs_t")
+        sl2_t = load_rows(sl2, "sl2_t")
+        th2_t = load_rows(th2, "th2_t")
+
+        def minus_product(slope, threshold, name):
+            product = pool.tile([P, PACK], F32, name=name + "_product")
+            nc.gpsimd.tensor_tensor(product[:], slope[:], threshold[:], MULT)
+            bias = pool.tile([P, PACK], F32, name=name)
+            nc.gpsimd.tensor_scalar(bias[:], product[:], -1.0, 0.0, MULT, ADD)
+            return bias
+
+        bias1 = minus_product(sl_t, th_t, "bias1")
+        bias2 = minus_product(sl2_t, th2_t, "bias2")
+
+        d_scale_picked = pool.tile([P, H], U8, name="d_scale_picked", align_bytes=64)
+        nc.vector.tensor_copy(d_scale_picked[:], d_scale_table[:].indirect(k1_t[:]))
+        d_scale_dealt = pool.tile([P, H], U8, name="d_scale_dealt", tag="page0", align_bytes=64)
+        nc.vector.tensor_copy(
+            d_scale_dealt[:].rearrange("p (t m) -> p t m", t=PACK), d_scale_picked[:].rearrange("p (m t) -> p t m", t=PACK)
+        )
+        nc.scalar.dma_start(d_scale[0:100, :].bitcast(I32), d_scale_dealt[14:114, :].bitcast(I32))
+
+        d_picked = pool.tile([P, H], U32, name="d_picked", align_bytes=64)
+        nc.vector.tensor_copy(d_picked[:], d_table[:].indirect(k1_t[:]))
+        d_codes = pool.tile([P, H], U32, name="d_codes", align_bytes=64)
+        nc.vector.tensor_copy(
+            d_codes[:].rearrange("p (t m) -> p m t", t=PACK), d_picked[:].rearrange("p (m t) -> p m t", t=PACK)
+        )
+        x_scale = pool.tile([P, S], U8, name="x_scale", tag="page3", align_bytes=64)
+        nc.vector.tensor_copy(x_scale[:], x_scale_table[:].indirect(offs_t[:]))
+        x_codes = pool.tile([P, S], U32, name="x_codes", tag="page2", align_bytes=64)
+        nc.vector.tensor_copy(x_codes[:], x_table[:].indirect(offs_t[:]))
+
+        def product(t, codes, scale, name):
+            acc = psum.tile([P, S], F32, name=name)
+            cols = slice(t * P, (t + 1) * P)
+            nc.tensor.matmul_mx(
+                out=acc[:],
+                lhsT=d_codes[:, cols].bitcast(FP8X4),
+                lhsT_scale=d_scale[:, cols],
+                rhs=codes[:].bitcast(FP8X4),
+                rhs_scale=scale[:],
+                start=True,
+                stop=True,
+            )
+            return acc
+
+        h = []
+        for t in range(PACK):
+            acc = product(t, x_codes, x_scale, f"acc_h{t}")
+            h_t = pool.tile([P, S], F32, name=f"h{t}")
+            nc.vector.tensor_scalar(h_t[:], acc[:], 0.0625, None, MULT)
+            h.append(h_t)
+
+        page = []
+        mem_rows = mem.rearrange("(p t) u -> t p u", t=PACK)
+        for t in range(PACK):
+            page_t = pool.tile([P, U], F32, name=f"page_{t}", tag=f"page{t}", align_bytes=64)
+            nc.sync.dma_start(page_t[:], mem_rows[t])
+            page.append(page_t)
+
+        ra, rb = [], []
+        for t in range(PACK):
+            one = slice(t, t + 1)
+            sg2 = pool.tile([P, W], F32, name=f"sg2_{t}")
+            nc.scalar.activation(sg2[:], h[t][:].indirect(n2_t[:]), SIGMOID, bias=bias1[:, one], scale=sl_t[:, one])
+            pa = pool.tile([P, W], F32, name=f"pa{t}")
+            nc.scalar.activation(pa[:], h[t][:].indirect(n1_t[:]), COPY)
+            sg = pool.tile([P, W], F32, name=f"sg{t}")
+            nc.scalar.activation(sg[:], h[t][:].indirect(n1_t[:]), SIGMOID, bias=bias1[:, one], scale=sl_t[:, one])
+            pb = pool.tile([P, W], F32, name=f"pb{t}")
+            nc.scalar.activation(pb[:], h[t][:].indirect(n2_t[:]), COPY)
+            ra_t = pool.tile([P, W], F32, name=f"ra{t}")
+            nc.vector.tensor_tensor(ra_t[:], pa[:], sg2[:], MULT)
+            rb_t = pool.tile([P, W], F32, name=f"rb{t}", tag=f"rb{t}")
+            nc.vector.tensor_tensor(rb_t[:], pb[:], sg[:], SUB)
+            ra.append(ra_t)
+            rb.append(rb_t)
+
+        dt = [pool.tile([P, S], F32, name=f"dt{t}", tag=f"dt{t}") for t in range(PACK)]
+        z = pool.tile([P, S, PACK], BF16, name="z", align_bytes=64)
+        for step in range(PACK + 1):
+            if step < PACK:
+                nc.scalar.activation(dt[step][:].indirect(n1_t[:]), ra[step][:], COPY)
+            if step > 0:
+                t = step - 1
+                nc.scalar.activation(dt[t][:].indirect(n2_t[:]), rb[t][:], COPY)
+                nc.vector.tensor_scalar(z[:, :, t], dt[t][:], gs_t[:, t : t + 1], None, MULT)
+
+        z_codes = pool.tile([P, S], U32, name="z_codes", align_bytes=64)
+        nc.vector.quantize_mx(out=z_codes[:].bitcast(FP8X4), scales=z_scale[:], in_=z[:].rearrange("p c t -> p (c t)"))
+
+        after = ["rb3", "rb2", "dt2", "dt3"]
+        both = [pool.tile([P, 2 * S], F32, name=f"h2_old{t}", tag=after[t]) for t in range(PACK)]
+        for t in range(PACK):
+            nc.scalar.activation(both[t][:, S:], page[t][:].indirect(n3_t[:]), COPY)
+
+        rounded = [pool.tile([P, HALF, PACK], BF16, name=f"rounded{a}", align_bytes=64) for a in range(2)]
+        out_rows = out_0.rearrange("(p t) u -> t p u", t=PACK)
+        nw = []
+
+        def gate(t):
+            one = slice(t, t + 1)
+            acc = product(t, z_codes, z_scale, f"acc_h2_{t}")
+            nc.vector.tensor_scalar(both[t][:, :S], acc[:], 0.0625, None, MULT)
+            sg3 = pool.tile([P, S], F32, name=f"sg3_{t}")
+            nc.scalar.activation(sg3[:], both[t][:].indirect(n4_t[:]), SIGMOID, bias=bias2[:, one], scale=sl2_t[:, one])
+            diff = pool.tile([P, S], F32, name=f"diff{t}")
+            nc.vector.tensor_tensor(diff[:], both[t][:, :S], both[t][:, S:], SUB)
+            pull = pool.tile([P, S], F32, name=f"pull{t}")
+            nc.vector.tensor_tensor(pull[:], sg3[:], diff[:], MULT)
+            nw_t = pool.tile([P, S], F32, name=f"nw{t}")
+            nc.vector.tensor_tensor(nw_t[:], both[t][:, S:], pull[:], ADD)
+            nw.append(nw_t)
+
+        def write(t):
+            nc.scalar.activation(page[t][:].indirect(n3_t[:]), nw[t][:], COPY)
+            nc.sync.dma_start(out_rows[t], page[t][:])
+            for a in range(2):
+                nc.vector.tensor_copy(rounded[a][:, :, t], page[t][:, a * HALF : (a + 1) * HALF])
+
+        for t in range(PACK):
+            gate(t)
+        for t in range(PACK):
+            write(t)
+
+        out_scale = pool.tile([P, U], U8, name="out_scale", align_bytes=64)
+        for a in range(2):
+            cols = slice(a * HALF, (a + 1) * HALF)
+            out_codes = pool.tile([P, HALF], U32, name=f"out_codes{a}", align_bytes=64)
+            nc.vector.quantize_mx(
+                out=out_codes[:].bitcast(FP8X4), scales=out_scale[:, cols], in_=rounded[a][:].rearrange("p c t -> p (c t)")
+            )
+            nc.sync.dma_start(words_of(out_1)[:, cols], out_codes[:].bitcast(I32))
+        out_scale_rows = out_2[0].bitcast(I32)
+        for q in range(4):
+            queue = nc.scalar if q % 2 == 0 else nc.sync
+            queue.dma_start(out_scale_rows[4 * q : 4 * q + 4, :], out_scale[32 * q : 32 * q + 4, :].bitcast(I32))

@@ -44,17 +44,22 @@ def tile_picked_ringeodepg_none_po_kernel(
             nc.sync.dma_start(tile[:], dram)
             return tile
 
-        def load_rows(dram, name):
-            tile = pool.tile([P, PACK], F32, name=name)
-            nc.gpsimd.dma_start(tile[:], dram.rearrange("(p t) o -> p (t o)", t=PACK))
+        def load_rows(queue, dram, name, tag=""):
+            tile = pool.tile([P, PACK], F32, name=name, tag=tag, align_bytes=64)
+            queue.dma_start(tile[:], dram.rearrange("(p t) o -> p (t o)", t=PACK))
             return tile
 
         d_scale_table = pool.tile([P, T], U8, name="d_scale_table", align_bytes=64)
-        d_scale_rows = d_scales[0].bitcast(I32).rearrange("(r e) c -> e r c", e=2)
-        for e in range(2):
-            nc.sync.dma_start(
-                d_scale_table[e:P:2, :].bitcast(I32), d_scale_rows[e].unsqueeze(1).to_broadcast([8, 8, T // 4])
-            )
+        nc.sync.dma_start(
+            d_scale_table[:].bitcast(I32), d_scales[0].bitcast(I32).unsqueeze(1).to_broadcast([16, 8, T // 4])
+        )
+        x_scale_table = pool.tile([P, T], U8, name="x_scale_table", tag="late2", align_bytes=64)
+        nc.gpsimd.memset(x_scale_table[:].bitcast(I32), 0)
+        x_scale_rows = x_scales[0].bitcast(I32)
+        for q in range(4):
+            queue = nc.gpsimd if q < 2 else nc.scalar
+            queue.dma_start(x_scale_table[32 * q : 32 * q + 4, :].bitcast(I32), x_scale_rows[4 * q : 4 * q + 4, :])
+
         k1_t = load_list(k1, "k1_t")
         offs_t = load_list(offs, "offs_t")
         n1_t = load_list(n1, "n1_t")
@@ -65,23 +70,18 @@ def tile_picked_ringeodepg_none_po_kernel(
         x_table = pool.tile([P, T], U32, name="x_table", tag="page1", align_bytes=64)
         nc.sync.dma_start(x_table[:].bitcast(I32), words_of(x_words))
         n4_t = load_list(n4, "n4_t")
-
-        x_scale_table = pool.tile([P, T], U8, name="x_scale_table", align_bytes=64)
-        nc.vector.memset(x_scale_table[:].bitcast(I32), 0)
-        x_scale_rows = x_scales[0].bitcast(I32)
-        for q in range(4):
-            nc.scalar.dma_start(x_scale_table[32 * q : 32 * q + 4, :].bitcast(I32), x_scale_rows[4 * q : 4 * q + 4, :])
+        sl_t = load_rows(nc.gpsimd, sl, "sl_t")
+        th_t = load_rows(nc.gpsimd, th, "th_t")
 
         d_scale = pool.tile([P, H], U8, name="d_scale", align_bytes=64)
         nc.vector.memset(d_scale[:].bitcast(I32), 0)
         z_scale = pool.tile([P, S], U8, name="z_scale", align_bytes=64)
         nc.vector.memset(z_scale[:].bitcast(I32), 0)
+        warm = pool.tile([P, 1], F32, name="warm")
+        nc.vector.memset(warm[:], 0.0)
+        warm_out = pool.tile([P, 1], F32, name="warm_out")
+        nc.scalar.activation(warm_out[:], warm[:], SIGMOID)
 
-        sl_t = load_rows(sl, "sl_t")
-        th_t = load_rows(th, "th_t")
-        gs_t = load_rows(gs, "gs_t")
-        sl2_t = load_rows(sl2, "sl2_t")
-        th2_t = load_rows(th2, "th2_t")
 
         def minus_product(slope, threshold, name):
             product = pool.tile([P, PACK], F32, name=name + "_product")
@@ -91,17 +91,20 @@ def tile_picked_ringeodepg_none_po_kernel(
             return bias
 
         bias1 = minus_product(sl_t, th_t, "bias1")
-        bias2 = minus_product(sl2_t, th2_t, "bias2")
 
-        d_scale_picked = pool.tile([P, H], U8, name="d_scale_picked", align_bytes=64)
+        d_scale_picked = pool.tile([P, H], U8, name="d_scale_picked", tag="late0", align_bytes=64)
         nc.vector.tensor_copy(d_scale_picked[:], d_scale_table[:].indirect(k1_t[:]))
         d_scale_dealt = pool.tile([P, H], U8, name="d_scale_dealt", tag="page0", align_bytes=64)
         nc.vector.tensor_copy(
             d_scale_dealt[:].rearrange("p (t m) -> p t m", t=PACK), d_scale_picked[:].rearrange("p (m t) -> p t m", t=PACK)
         )
-        nc.scalar.dma_start(d_scale[0:100, :].bitcast(I32), d_scale_dealt[14:114, :].bitcast(I32))
+        for q in range(4):
+            queue = nc.scalar if q % 2 == 0 else nc.sync
+            queue.dma_start(
+                d_scale[32 * q : 32 * q + 4, :].bitcast(I32), d_scale_dealt[32 * q : 32 * q + 32 : 8, :].bitcast(I32)
+            )
 
-        d_picked = pool.tile([P, H], U32, name="d_picked", align_bytes=64)
+        d_picked = pool.tile([P, H], U32, name="d_picked", tag="late1", align_bytes=64)
         nc.vector.tensor_copy(d_picked[:], d_table[:].indirect(k1_t[:]))
         d_codes = pool.tile([P, H], U32, name="d_codes", align_bytes=64)
         nc.vector.tensor_copy(
@@ -111,6 +114,11 @@ def tile_picked_ringeodepg_none_po_kernel(
         nc.vector.tensor_copy(x_scale[:], x_scale_table[:].indirect(offs_t[:]))
         x_codes = pool.tile([P, S], U32, name="x_codes", tag="page2", align_bytes=64)
         nc.vector.tensor_copy(x_codes[:], x_table[:].indirect(offs_t[:]))
+
+        gs_t = load_rows(nc.gpsimd, gs, "gs_t", "late0")
+        sl2_t = load_rows(nc.gpsimd, sl2, "sl2_t", "late1")
+        th2_t = load_rows(nc.gpsimd, th2, "th2_t", "late2")
+        bias2 = minus_product(sl2_t, th2_t, "bias2")
 
         def product(t, codes, scale, name):
             acc = psum.tile([P, S], F32, name=name)
@@ -176,20 +184,30 @@ def tile_picked_ringeodepg_none_po_kernel(
         for t in range(PACK):
             nc.scalar.activation(both[t][:, S:], page[t][:].indirect(n3_t[:]), COPY)
 
-        rounded = [pool.tile([P, HALF, PACK], BF16, name=f"rounded{a}", align_bytes=64) for a in range(2)]
+        pieces = [slice(0, 512), slice(512, 768), slice(768, U)]
+        rounded = [
+            pool.tile([P, cols.stop - cols.start, PACK], BF16, name=f"rounded{a}", align_bytes=64)
+            for a, cols in enumerate(pieces)
+        ]
+        staged = pool.tile([P, PACK, 256], BF16, name="staged", align_bytes=64)
         out_rows = out_0.rearrange("(p t) u -> t p u", t=PACK)
         nw = []
 
-        def gate(t):
+        acc2, sg3 = [], []
+        for t in range(PACK):
             one = slice(t, t + 1)
             acc = product(t, z_codes, z_scale, f"acc_h2_{t}")
             nc.vector.tensor_scalar(both[t][:, :S], acc[:], 0.0625, None, MULT)
-            sg3 = pool.tile([P, S], F32, name=f"sg3_{t}")
-            nc.scalar.activation(sg3[:], both[t][:].indirect(n4_t[:]), SIGMOID, bias=bias2[:, one], scale=sl2_t[:, one])
+            sg3_t = pool.tile([P, S], F32, name=f"sg3_{t}")
+            nc.scalar.activation(sg3_t[:], both[t][:].indirect(n4_t[:]), SIGMOID, bias=bias2[:, one], scale=sl2_t[:, one])
+            acc2.append(acc)
+            sg3.append(sg3_t)
+
+        def gate(t):
             diff = pool.tile([P, S], F32, name=f"diff{t}")
-            nc.vector.tensor_tensor(diff[:], both[t][:, :S], both[t][:, S:], SUB)
+            nc.vector.scalar_tensor_tensor(diff[:], acc2[t][:], 0.0625, both[t][:, S:], MULT, SUB)
             pull = pool.tile([P, S], F32, name=f"pull{t}")
-            nc.vector.tensor_tensor(pull[:], sg3[:], diff[:], MULT)
+            nc.vector.tensor_tensor(pull[:], sg3[t][:], diff[:], MULT)
             nw_t = pool.tile([P, S], F32, name=f"nw{t}")
             nc.vector.tensor_tensor(nw_t[:], both[t][:, S:], pull[:], ADD)
             nw.append(nw_t)
@@ -198,7 +216,14 @@ def tile_picked_ringeodepg_none_po_kernel(
             nc.scalar.activation(page[t][:].indirect(n3_t[:]), nw[t][:], COPY)
             nc.sync.dma_start(out_rows[t], page[t][:])
             for a in range(2):
-                nc.vector.tensor_copy(rounded[a][:, :, t], page[t][:, a * HALF : (a + 1) * HALF])
+                nc.vector.tensor_copy(rounded[a][:, :, t], page[t][:, pieces[a]])
+            if t < PACK - 1:
+                nc.vector.tensor_copy(staged[:, t, :], page[t][:, pieces[2]])
+            else:
+                nc.scalar.copy(staged[:, t, :], page[t][:, pieces[2]])
+                nc.scalar.copy(
+                    rounded[2][:].rearrange("p (c i) t -> p c t i", i=4), staged[:].rearrange("p t (c i) -> p c t i", i=4)
+                )
 
         for t in range(PACK):
             gate(t)
@@ -206,9 +231,8 @@ def tile_picked_ringeodepg_none_po_kernel(
             write(t)
 
         out_scale = pool.tile([P, U], U8, name="out_scale", align_bytes=64)
-        for a in range(2):
-            cols = slice(a * HALF, (a + 1) * HALF)
-            out_codes = pool.tile([P, HALF], U32, name=f"out_codes{a}", align_bytes=64)
+        for a, cols in enumerate(pieces):
+            out_codes = pool.tile([P, cols.stop - cols.start], U32, name=f"out_codes{a}", align_bytes=64)
             nc.vector.quantize_mx(
                 out=out_codes[:].bitcast(FP8X4), scales=out_scale[:, cols], in_=rounded[a][:].rearrange("p c t -> p (c t)")
             )

from contextlib import ExitStack

import concourse.mybir as mybir

F32 = mybir.dt.float32
BF16 = mybir.dt.bfloat16
I32 = mybir.dt.int32
U32 = mybir.dt.uint32
U16 = mybir.dt.uint16
U8 = mybir.dt.uint8
FP8X4 = mybir.dt.float8_e4m3fn_x4
MULT = mybir.AluOpType.mult
ADD = mybir.AluOpType.add
SUB = mybir.AluOpType.subtract
COPY = mybir.ActivationFunctionType.Copy
SIGMOID = mybir.ActivationFunctionType.Sigmoid

P = 128
PACK = 4
T = 2048
S = 256
H = 512
W = 128
U = 1024
HALF = U // 2
FLOPS = 2 * 2 * 512 * H * S


def words_of(dram):
    return dram[0].rearrange("p c r -> p (c r)").bitcast(I32)


def tile_picked_ringeodepg_none_po_kernel(
    tc, x_words, x_scales, d_words, d_scales, sl, th, gs, mem, sl2, th2, offs, k1, n1, n2, n3, n4, out_0, out_1, out_2
):
    nc = tc.nc
    with ExitStack() as ctx:
        lists = ctx.enter_context(tc.tile_pool(name="lists", bufs=1))
        pool = ctx.enter_context(tc.tile_pool(name="pool", bufs=1))
        psum = ctx.enter_context(tc.psum_pool(name="psum", bufs=1))

        def load_list(dram, name):
            tile = lists.tile(list(dram.shape), U16, name=name)
            nc.sync.dma_start(tile[:], dram)
            return tile

        def load_rows(queue, dram, name, tag=""):
            tile = pool.tile([P, PACK], F32, name=name, tag=tag, align_bytes=64)
            queue.dma_start(tile[:], dram.rearrange("(p t) o -> p (t o)", t=PACK))
            return tile

        d_scale_table = pool.tile([P, T], U8, name="d_scale_table", align_bytes=64)
        nc.sync.dma_start(
            d_scale_table[:].bitcast(I32), d_scales[0].bitcast(I32).unsqueeze(1).to_broadcast([16, 8, T // 4])
        )
        x_scale_table = pool.tile([P, T], U8, name="x_scale_table", tag="late2", align_bytes=64)
        nc.gpsimd.memset(x_scale_table[:].bitcast(I32), 0)
        x_scale_rows = x_scales[0].bitcast(I32)
        for q in range(4):
            queue = nc.gpsimd if q < 2 else nc.scalar
            queue.dma_start(x_scale_table[32 * q : 32 * q + 4, :].bitcast(I32), x_scale_rows[4 * q : 4 * q + 4, :])

        k1_t = load_list(k1, "k1_t")
        offs_t = load_list(offs, "offs_t")
        n1_t = load_list(n1, "n1_t")
        n2_t = load_list(n2, "n2_t")
        n3_t = load_list(n3, "n3_t")
        d_table = pool.tile([P, T], U32, name="d_table", tag="page3", align_bytes=64)
        nc.sync.dma_start(d_table[:].bitcast(I32), words_of(d_words))
        x_table = pool.tile([P, T], U32, name="x_table", tag="page1", align_bytes=64)
        nc.sync.dma_start(x_table[:].bitcast(I32), words_of(x_words))
        n4_t = load_list(n4, "n4_t")
        sl_t = load_rows(nc.gpsimd, sl, "sl_t")
        th_t = load_rows(nc.gpsimd, th, "th_t")

        d_scale = pool.tile([P, H], U8, name="d_scale", align_bytes=64)
        nc.vector.memset(d_scale[:].bitcast(I32), 0)
        z_scale = pool.tile([P, S], U8, name="z_scale", align_bytes=64)
        nc.vector.memset(z_scale[:].bitcast(I32), 0)
        warm = pool.tile([P, 1], F32, name="warm")
        nc.vector.memset(warm[:], 0.0)
        warm_out = pool.tile([P, 1], F32, name="warm_out")
        nc.scalar.activation(warm_out[:], warm[:], SIGMOID)


        def minus_product(slope, threshold, name):
            product = pool.tile([P, PACK], F32, name=name + "_product")
            nc.gpsimd.tensor_tensor(product[:], slope[:], threshold[:], MULT)
            bias = pool.tile([P, PACK], F32, name=name)
            nc.gpsimd.tensor_scalar(bias[:], product[:], -1.0, 0.0, MULT, ADD)
            return bias

        bias1 = minus_product(sl_t, th_t, "bias1")

        d_scale_picked = pool.tile([P, H], U8, name="d_scale_picked", tag="late0", align_bytes=64)
        nc.vector.tensor_copy(d_scale_picked[:], d_scale_table[:].indirect(k1_t[:]))
        d_scale_dealt = pool.tile([P, H], U8, name="d_scale_dealt", tag="page0", align_bytes=64)
        nc.vector.tensor_copy(
            d_scale_dealt[:].rearrange("p (t m) -> p t m", t=PACK), d_scale_picked[:].rearrange("p (m t) -> p t m", t=PACK)
        )
        for q in range(4):
            queue = nc.scalar if q % 2 == 0 else nc.sync
            queue.dma_start(
                d_scale[32 * q : 32 * q + 4, :].bitcast(I32), d_scale_dealt[32 * q : 32 * q + 32 : 8, :].bitcast(I32)
            )

        d_picked = pool.tile([P, H], U32, name="d_picked", tag="late1", align_bytes=64)
        nc.vector.tensor_copy(d_picked[:], d_table[:].indirect(k1_t[:]))
        d_codes = pool.tile([P, H], U32, name="d_codes", align_bytes=64)
        nc.vector.tensor_copy(
            d_codes[:].rearrange("p (t m) -> p m t", t=PACK), d_picked[:].rearrange("p (m t) -> p m t", t=PACK)
        )
        x_scale = pool.tile([P, S], U8, name="x_scale", tag="page3", align_bytes=64)
        nc.vector.tensor_copy(x_scale[:], x_scale_table[:].indirect(offs_t[:]))
        x_codes = pool.tile([P, S], U32, name="x_codes", tag="page2", align_bytes=64)
        nc.vector.tensor_copy(x_codes[:], x_table[:].indirect(offs_t[:]))

        gs_t = load_rows(nc.gpsimd, gs, "gs_t", "late0")
        sl2_t = load_rows(nc.gpsimd, sl2, "sl2_t", "late1")
        th2_t = load_rows(nc.gpsimd, th2, "th2_t", "late2")
        bias2 = minus_product(sl2_t, th2_t, "bias2")

        def product(t, codes, scale, name):
            acc = psum.tile([P, S], F32, name=name)
            cols = slice(t * P, (t + 1) * P)
            nc.tensor.matmul_mx(
                out=acc[:],
                lhsT=d_codes[:, cols].bitcast(FP8X4),
                lhsT_scale=d_scale[:, cols],
                rhs=codes[:].bitcast(FP8X4),
                rhs_scale=scale[:],
                start=True,
                stop=True,
            )
            return acc

        h = []
        for t in range(PACK):
            acc = product(t, x_codes, x_scale, f"acc_h{t}")
            h_t = pool.tile([P, S], F32, name=f"h{t}")
            nc.vector.tensor_scalar(h_t[:], acc[:], 0.0625, None, MULT)
            h.append(h_t)

        page = []
        mem_rows = mem.rearrange("(p t) u -> t p u", t=PACK)
        for t in range(PACK):
            page_t = pool.tile([P, U], F32, name=f"page_{t}", tag=f"page{t}", align_bytes=64)
            nc.sync.dma_start(page_t[:], mem_rows[t])
            page.append(page_t)

        ra, rb = [], []
        for t in range(PACK):
            one = slice(t, t + 1)
            sg2 = pool.tile([P, W], F32, name=f"sg2_{t}")
            nc.scalar.activation(sg2[:], h[t][:].indirect(n2_t[:]), SIGMOID, bias=bias1[:, one], scale=sl_t[:, one])
            pa = pool.tile([P, W], F32, name=f"pa{t}")
            nc.scalar.activation(pa[:], h[t][:].indirect(n1_t[:]), COPY)
            sg = pool.tile([P, W], F32, name=f"sg{t}")
            nc.scalar.activation(sg[:], h[t][:].indirect(n1_t[:]), SIGMOID, bias=bias1[:, one], scale=sl_t[:, one])
            pb = pool.tile([P, W], F32, name=f"pb{t}")
            nc.scalar.activation(pb[:], h[t][:].indirect(n2_t[:]), COPY)
            ra_t = pool.tile([P, W], F32, name=f"ra{t}")
            nc.vector.tensor_tensor(ra_t[:], pa[:], sg2[:], MULT)
            rb_t = pool.tile([P, W], F32, name=f"rb{t}", tag=f"rb{t}")
            nc.vector.tensor_tensor(rb_t[:], pb[:], sg[:], SUB)
            ra.append(ra_t)
            rb.append(rb_t)

        dt = [pool.tile([P, S], F32, name=f"dt{t}", tag=f"dt{t}") for t in range(PACK)]
        z = pool.tile([P, S, PACK], BF16, name="z", align_bytes=64)
        for step in range(PACK + 1):
            if step < PACK:
                nc.scalar.activation(dt[step][:].indirect(n1_t[:]), ra[step][:], COPY)
            if step > 0:
                t = step - 1
                nc.scalar.activation(dt[t][:].indirect(n2_t[:]), rb[t][:], COPY)
                nc.vector.tensor_scalar(z[:, :, t], dt[t][:], gs_t[:, t : t + 1], None, MULT)

        z_codes = pool.tile([P, S], U32, name="z_codes", align_bytes=64)
        nc.vector.quantize_mx(out=z_codes[:].bitcast(FP8X4), scales=z_scale[:], in_=z[:].rearrange("p c t -> p (c t)"))

        after = ["rb3", "rb2", "dt2", "dt3"]
        both = [pool.tile([P, 2 * S], F32, name=f"h2_old{t}", tag=after[t]) for t in range(PACK)]
        for t in range(PACK):
            nc.scalar.activation(both[t][:, S:], page[t][:].indirect(n3_t[:]), COPY)

        pieces = [slice(0, 512), slice(512, 768), slice(768, U)]
        rounded = [
            pool.tile([P, cols.stop - cols.start, PACK], BF16, name=f"rounded{a}", align_bytes=64)
            for a, cols in enumerate(pieces)
        ]
        staged = pool.tile([P, PACK, 256], BF16, name="staged", align_bytes=64)
        out_rows = out_0.rearrange("(p t) u -> t p u", t=PACK)
        nw = []

        acc2, sg3 = [], []
        for t in range(PACK):
            one = slice(t, t + 1)
            acc = product(t, z_codes, z_scale, f"acc_h2_{t}")
            nc.vector.tensor_scalar(both[t][:, :S], acc[:], 0.0625, None, MULT)
            sg3_t = pool.tile([P, S], F32, name=f"sg3_{t}")
            nc.scalar.activation(sg3_t[:], both[t][:].indirect(n4_t[:]), SIGMOID, bias=bias2[:, one], scale=sl2_t[:, one])
            acc2.append(acc)
            sg3.append(sg3_t)

        def gate(t):
            diff = pool.tile([P, S], F32, name=f"diff{t}")
            nc.vector.scalar_tensor_tensor(diff[:], acc2[t][:], 0.0625, both[t][:, S:], MULT, SUB)
            pull = pool.tile([P, S], F32, name=f"pull{t}")
            nc.vector.tensor_tensor(pull[:], sg3[t][:], diff[:], MULT)
            nw_t = pool.tile([P, S], F32, name=f"nw{t}")
            nc.vector.tensor_tensor(nw_t[:], both[t][:, S:], pull[:], ADD)
            nw.append(nw_t)

        def write(t):
            nc.scalar.activation(page[t][:].indirect(n3_t[:]), nw[t][:], COPY)
            nc.sync.dma_start(out_rows[t], page[t][:])
            for a in range(2):
                nc.vector.tensor_copy(rounded[a][:, :, t], page[t][:, pieces[a]])
            if t < PACK - 1:
                nc.vector.tensor_copy(staged[:, t, :], page[t][:, pieces[2]])
            else:
                nc.scalar.copy(staged[:, t, :], page[t][:, pieces[2]])
                nc.scalar.copy(
                    rounded[2][:].rearrange("p (c i) t -> p c t i", i=4), staged[:].rearrange("p t (c i) -> p c t i", i=4)
                )

        for t in range(PACK):
            gate(t)
        for t in range(PACK):
            write(t)

        out_scale = pool.tile([P, U], U8, name="out_scale", align_bytes=64)
        for a, cols in enumerate(pieces):
            out_codes = pool.tile([P, cols.stop - cols.start], U32, name=f"out_codes{a}", align_bytes=64)
            nc.vector.quantize_mx(
                out=out_codes[:].bitcast(FP8X4), scales=out_scale[:, cols], in_=rounded[a][:].rearrange("p c t -> p (c t)")
            )
            nc.sync.dma_start(words_of(out_1)[:, cols], out_codes[:].bitcast(I32))
        out_scale_rows = out_2[0].bitcast(I32)
        for q in range(4):
            queue = nc.scalar if q % 2 == 0 else nc.sync
            queue.dma_start(out_scale_rows[4 * q : 4 * q + 4, :], out_scale[32 * q : 32 * q + 4, :].bitcast(I32))
